import numpy as np
import ml_dtypes


def mxq(x, axis, fmt="e4m3"):
    dtype, down = {"e4m3": (ml_dtypes.float8_e4m3fn, 7), "e5m2": (ml_dtypes.float8_e5m2, 14)}[fmt]
    v = np.moveaxis(np.asarray(x, np.float32).astype(ml_dtypes.bfloat16).astype(np.float64), axis, -1)
    blocks = v.reshape(v.shape[:-1] + (-1, 32))
    amax = np.abs(blocks).max(-1, keepdims=True)
    byte = np.maximum(np.where(amax > 0, np.frexp(amax)[1] - 1 + 127, 0) - down, 1)
    scale = np.exp2(byte - 127.0)
    codes = (blocks / scale).astype(np.float32).astype(dtype).astype(np.float64)
    return np.moveaxis((codes * scale).reshape(v.shape), -1, axis)


WIDE = False


def mx_kscale(k):
    if not WIDE:
        return np.ones(k)
    levels = np.array([10, -10, 5, -5, 0])
    if k % 512:
        return np.exp2(np.random.permutation(np.resize(levels, k // 32))).repeat(32)
    a = np.empty((k // 512, 16))
    for p in range(k // 512):
        a[p, :8] = np.random.permutation(np.resize(levels, 8))
        for g in range(8):
            far = levels[np.abs(levels - a[p, g]) >= 10]
            a[p, g + 8] = far[np.random.randint(len(far))]
    return np.exp2(a.ravel()).repeat(32)


def f64(x):
    return np.asarray(x).astype(np.float64)


def striped(idx):
    return np.tile(idx.reshape(-1, 16).T, (8, 1)).astype(np.uint16)


def unstriped(offs):
    return offs[:16].T.reshape(-1).astype(np.int64)


def striped8(idx):
    return np.concatenate([x.reshape(-1, 16).T for x in idx]).astype(np.uint16)


def runs(offs, k):
    lists = np.stack([offs[16 * r : 16 * r + 16].T.reshape(-1) for r in range(8)]).astype(np.int64)
    return lists[np.arange(k) % 512 // 64]


def pack_weight(w):
    k, n = w.shape
    w = f64(np.asarray(w, np.float32).astype(ml_dtypes.bfloat16)).reshape(k // 32, 32, n)
    amax = np.abs(w).max(1)
    byte = np.clip(np.where(amax > 0, np.frexp(amax)[1] - 1 + 127 - 7, 1), 1, 254)
    scaled = (w * np.exp2(127.0 - byte)[:, None, :]).reshape(k, n).astype(np.float32)
    words = np.ascontiguousarray(scaled.reshape(k // 512, 128, 4, n).transpose(0, 1, 3, 2)).astype(ml_dtypes.float8_e4m3fn).view(np.uint8)
    return words, np.ascontiguousarray(byte.astype(np.uint8).reshape(k // 512, 16, n))


def unpack_weight(words, scales):
    g, p, n, _ = words.shape
    vals = np.ascontiguousarray(words).view(ml_dtypes.float8_e4m3fn).astype(np.float64) * np.repeat(np.exp2(scales.astype(np.float64) - 127.0), 8, axis=1)[..., None]
    return vals.transpose(0, 1, 3, 2).reshape(g * 512, n)


def sigmoid(v):
    return 1.0 / (1.0 + np.exp(-np.maximum(v, -700.0)))


K, T, S, V, H, J = 512, 2048, 512, 512, 512, 512


def setup_inputs():
    n = np.random.standard_normal
    s = mx_kscale(K)[:, None]
    u = mx_kscale(S)
    packed_xT = pack_weight(n((K, T)) * s)
    return {
        "x_words": packed_xT[0],
        "x_scales": packed_xT[1],
        "w1": (n((K, H)) / np.sqrt(K) / s).astype(np.float32),
        "w2": (n((K, H)) / np.sqrt(K) / s).astype(np.float32),
        "ga": (np.random.uniform(0.5, 1.5, (H, 1)) * u[:, None]).astype(np.float32),
        "gb": (np.random.uniform(0.5, 1.5, (H, 1)) / u[:, None]).astype(np.float32),
        "tab": n((S, J)).astype(np.float32),
        "offs": striped(np.random.permutation(T)[:S]),
        "two": striped(np.random.permutation(T)[:V]),
        "n1": striped8(np.stack([np.random.permutation(S) for _ in range(8)])),
        "n2": striped8(np.stack([np.random.permutation(S) for _ in range(8)])),
        "n3": striped8(np.stack([np.random.permutation(V) for _ in range(8)])),
        "n4": striped8(np.random.randint(0, J, (8, V))),
        "n5": striped8(np.stack([np.random.permutation(V) for _ in range(8)])),
    }


def reference(x_words, x_scales, w1, w2, ga, gb, tab, offs, two, n1, n2, n3, n4, n5):
    xq = unpack_weight(x_words, x_scales)[:, unstriped(offs)]
    a = mxq(f64(w1), 0, "e4m3").T @ xq
    pa = a[np.arange(H)[:, None], runs(n1, H)]
    pb = a[np.arange(H)[:, None], runs(n2, H)]
    mu = 0.3125 * (a + pa + pb)
    z = f64(ga) * ((a - mu) / (np.sqrt((pa - mu) ** 2 + (pb - mu) ** 2 + 0.25)))
    x_two = unpack_weight(x_words, x_scales)[:, unstriped(two)]
    b = mxq(f64(w2), 0, "e4m3").T @ x_two
    st = b * (sigmoid(b[np.arange(H)[:, None], runs(n3, H)]))
    z2 = f64(gb) * (np.maximum(st, st[np.arange(H)[:, None], runs(n3, H)]))
    s = 0.0625 * ((mxq(z, 0, "e4m3").T @ mxq(z2, 0, "e4m3")))
    return np.maximum(s + f64(tab)[np.arange(S)[:, None], runs(n4, S)], s[np.arange(S)[:, None], runs(n5, S)])

@@ -1,0 +1,211 @@
+from contextlib import ExitStack
+
+import concourse.mybir as mybir
+from concourse.masks import make_identity
+
+F32 = mybir.dt.float32
+BF16 = mybir.dt.bfloat16
+I32 = mybir.dt.int32
+U32 = mybir.dt.uint32
+U16 = mybir.dt.uint16
+U8 = mybir.dt.uint8
+FP8X4 = mybir.dt.float8_e4m3fn_x4
+ALU = mybir.AluOpType
+ACT = mybir.ActivationFunctionType
+
+P = 128
+PACK = 4
+N = 512
+T = 2048
+WIN = 2 * N
+C = 0.3125
+FLOPS = 3 * 2 * 512 * 512 * 512
+
+
+def tile_picked_kqstdtwicpkind_none_p_kernel(tc, x_words, x_scales, w1, w2, ga, gb, tab, offs, two, n1, n2, n3, n4, n5, out):
+    nc = tc.nc
+    with ExitStack() as ctx:
+        keep = ctx.enter_context(tc.tile_pool(name="keep", bufs=1))
+        ring = ctx.enter_context(tc.tile_pool(name="ring", bufs=2))
+        psum = ctx.enter_context(tc.psum_pool(name="psum", bufs=2))
+
+        def list_tile(name):
+            return keep.tile([P, N // 16], U16, name=name)
+
+        l_offs, l_two, l_n1, l_n2, l_n3, l_n4, l_n5 = [list_tile(n) for n in ("l_offs", "l_two", "l_n1", "l_n2", "l_n3", "l_n4", "l_n5")]
+        xs = keep.tile([P, T], U8, name="xs", align_bytes=64)
+        xw = keep.tile([P, T], U32, name="xw", align_bytes=64)
+        w1_raw = keep.tile([P, PACK, N], F32, name="w1_raw")
+        w2_raw = keep.tile([P, PACK, N], F32, name="w2_raw")
+        a_win = [keep.tile([P, WIN], F32, name="a_win%d" % t) for t in range(PACK)]
+        b_win = [keep.tile([P, WIN], F32, name="b_win%d" % t) for t in range(PACK)]
+        st_win = [keep.tile([P, WIN], F32, name="st_win%d" % t) for t in range(PACK)]
+        tab_win = [keep.tile([P, WIN], F32, name="tab_win%d" % t) for t in range(PACK)]
+        ga_sb = keep.tile([P, PACK], F32, name="ga_sb")
+        gb_sb = keep.tile([P, PACK], F32, name="gb_sb")
+        quarter = keep.tile([P, 1], F32, name="quarter")
+        warm = keep.tile([P, 1], F32, name="warm")
+        ident = keep.tile([P, P], F32, name="ident")
+
+        nc.vector.memset(xs[:].bitcast(I32), 0)
+        nc.vector.memset(quarter[:], 0.25)
+        nc.scalar.activation(out=warm[:], in_=quarter[:], func=ACT.Sigmoid)
+        nc.sync.dma_start(l_offs[:], offs)
+        nc.sync.dma_start(l_two[:], two)
+        for q in range(4):
+            nc.sync.dma_start(out=xs[32 * q : 32 * q + 4, :].bitcast(I32), in_=x_scales[0, 4 * q : 4 * q + 4, :].bitcast(I32))
+        nc.sync.dma_start(out=w1_raw[:], in_=w1.rearrange("(p j) c -> p j c", j=PACK))
+        nc.sync.dma_start(out=xw[:].bitcast(I32), in_=x_words[0].rearrange("p n t -> p (n t)").bitcast(I32))
+        nc.sync.dma_start(out=w2_raw[:], in_=w2.rearrange("(p j) c -> p j c", j=PACK))
+        nc.sync.dma_start(l_n1[:], n1)
+        nc.sync.dma_start(l_n2[:], n2)
+        nc.sync.dma_start(l_n3[:], n3)
+        nc.sync.dma_start(out=ga_sb[:], in_=ga.rearrange("(p t) o -> p (t o)", t=PACK))
+        nc.sync.dma_start(out=gb_sb[:], in_=gb.rearrange("(p t) o -> p (t o)", t=PACK))
+        make_identity(nc, ident[:])
+        tab_rows = tab.rearrange("(p t) v -> p t v", t=PACK)
+        for t in range(PACK):
+            nc.sync.dma_start(out=tab_win[t][:, :N], in_=tab_rows[:, t, :])
+        nc.sync.dma_start(l_n4[:], n4)
+        nc.sync.dma_start(l_n5[:], n5)
+        for t in range(PACK):
+            nc.vector.memset(b_win[t][:, N:], 0.0)
+        for t in range(PACK):
+            nc.vector.memset(tab_win[t][:, N:], 0.0)
+
+        xa_s = keep.tile([P, N], U8, name="xa_s", align_bytes=64)
+        xb_s = keep.tile([P, N], U8, name="xb_s", align_bytes=64)
+        xa_w = keep.tile([P, N], U32, name="xa_w", align_bytes=64)
+        xb_w = keep.tile([P, N], U32, name="xb_w", align_bytes=64)
+        nc.vector.tensor_copy(xa_s[:], xs[:].indirect(l_offs[:]))
+        nc.vector.tensor_copy(xb_s[:], xs[:].indirect(l_two[:]))
+
+        twice_pos = keep.tile([P, PACK], F32, name="twice_pos")
+        gb_abs = keep.tile([P, PACK], F32, name="gb_abs")
+        ga_sgn = keep.tile([P, PACK], F32, name="ga_sgn")
+        ga_z = keep.tile([P, PACK], F32, name="ga_z")
+
+        def deal(engine_copy, dst, src, half):
+            ms = slice(half * 64, (half + 1) * 64)
+            engine_copy(
+                dst[:].rearrange("p (t m j) -> p m j t", t=PACK, j=PACK)[:, ms, :, :],
+                src.rearrange("p j (m t) -> p m j t", t=PACK)[:, ms, :, :],
+            )
+
+        def quantise(name, grouped):
+            codes = keep.tile([P, N], U32, name=name + "_c", align_bytes=64)
+            scales = keep.tile([P, N], U8, name=name + "_s", align_bytes=64)
+            nc.vector.quantize_mx(out=codes[:].bitcast(FP8X4), scales=scales[:], in_=grouped[:])
+            return codes, scales
+
+        def product(lhs, t, rhs_c, rhs_s):
+            acc = psum.tile([P, N], F32, name="acc")
+            cols = slice(t * P, (t + 1) * P)
+            nc.tensor.matmul_mx(out=acc[:], lhsT=lhs[0][:, cols].bitcast(FP8X4), lhsT_scale=lhs[1][:, cols],
+                                rhs=rhs_c[:].bitcast(FP8X4), rhs_scale=rhs_s[:], start=True, stop=True)
+            return acc
+
+        def turned_sum(name, terms):
+            acc = psum.tile([P, N], F32, name=name)
+            for k in range(PACK):
+                cols = slice(k * P, (k + 1) * P)
+                for i, term in enumerate(terms):
+                    nc.tensor.matmul(acc[:, cols], term[:, cols], ident[:], start=(i == 0), stop=(i == len(terms) - 1), is_transpose=True)
+            return acc
+
+        w1_g = keep.tile([P, PACK * N], BF16, name="w1_g", align_bytes=64)
+        w2_g = keep.tile([P, PACK * N], BF16, name="w2_g", align_bytes=64)
+        deal(nc.scalar.copy, w1_g, w1_raw[:], 0)
+        deal(nc.vector.tensor_copy, w1_g, w1_raw[:], 1)
+        w1_q = quantise("w1q", w1_g)
+        nc.vector.tensor_copy(xa_w[:], xw[:].indirect(l_offs[:]))
+        nc.vector.tensor_copy(xb_w[:], xw[:].indirect(l_two[:]))
+
+        num = keep.tile([P, PACK, N], F32, name="num")
+        sq_d = keep.tile([P, PACK, N], F32, name="sq_d")
+        sq_e = keep.tile([P, PACK, N], F32, name="sq_e")
+        zb = keep.tile([P, PACK, N], BF16, name="zb")
+        z2b = keep.tile([P, PACK, N], BF16, name="z2b")
+
+        def a_out(t):
+            acc = product(w1_q, t, xa_w, xa_s)
+            nc.scalar.copy(a_win[t][:, :N], acc[:])
+            nc.scalar.activation(out=a_win[t][:, N:], in_=acc[:], func=ACT.Copy, scale=-2.0 * C / (1.0 - 2.0 * C))
+
+        def a_gather(t):
+            pa = ring.tile([P, N], F32, name="pa")
+            diff = ring.tile([P, N], F32, name="diff")
+            both = ring.tile([P, N], F32, name="both")
+            nc.vector.tensor_copy(pa[:], a_win[t][:].indirect(l_n1[:]))
+            nc.vector.tensor_tensor(diff[:], a_win[t][:].indirect(l_n2[:]), pa[:], ALU.subtract)
+            nc.vector.scalar_tensor_tensor(both[:], pa[:], 2.0, diff[:], ALU.mult, ALU.add)
+            nc.vector.scalar_tensor_tensor(num[:, t, :], both[:], -C / (1.0 - C), a_win[t][:, :N], ALU.mult, ALU.add)
+            d_t = turned_sum("d_t", [diff])
+            e_t = turned_sum("e_t", [both, a_win[t][:, N:]])
+            nc.scalar.activation(out=sq_d[:, t, :], in_=d_t[:], func=ACT.Square)
+            nc.scalar.activation(out=sq_e[:, t, :], in_=e_t[:], func=ACT.Square, scale=1.0 - 2.0 * C)
+
+        def b_out(t, w2_q):
+            acc = product(w2_q, t, xb_w, xb_s)
+            nc.scalar.copy(b_win[t][:, :N], acc[:])
+            nc.scalar.activation(out=st_win[t][:, N:], in_=b_win[t][:].indirect(l_n3[:]), func=ACT.Sigmoid)
+
+        def b_gather(t):
+            other = ring.tile([P, N], F32, name="other")
+            nc.vector.scalar_tensor_tensor(st_win[t][:, :N], b_win[t][:, :N], gb_abs[:, t : t + 1], st_win[t][:, N:], ALU.mult, ALU.mult)
+            nc.vector.tensor_copy(other[:], st_win[t][:].indirect(l_n3[:]))
+            nc.vector.tensor_tensor(z2b[:, t, :], other[:], st_win[t][:, :N], ALU.max)
+
+        def a_finish(t):
+            den = turned_sum("den", [sq_d[:, t, :], sq_e[:, t, :]])
+            rs = ring.tile([P, N], F32, name="rs")
+            nc.scalar.activation(out=rs[:], in_=den[:], func=ACT.Abs_reciprocal_sqrt, bias=quarter[:], scale=0.5)
+            nc.vector.scalar_tensor_tensor(zb[:, t, :], num[:, t, :], ga_z[:, t : t + 1], rs[:], ALU.mult, ALU.mult)
+
+        a_out(0)
+        a_out(1)
+        deal(nc.scalar.copy, w2_g, w2_raw[:], 0)
+        deal(nc.scalar.copy, w2_g, w2_raw[:], 1)
+        a_gather(0)
+        a_out(2)
+        w2_q = quantise("w2q", w2_g)
+        a_gather(1)
+        a_out(3)
+        b_out(0, w2_q)
+        a_gather(2)
+        b_out(1, w2_q)
+        a_gather(3)
+        b_out(2, w2_q)
+        b_out(3, w2_q)
+        nc.vector.tensor_scalar(twice_pos[:], gb_sb[:], 0.0, 2.0, ALU.is_ge, ALU.mult)
+        nc.vector.scalar_tensor_tensor(gb_abs[:], twice_pos[:], -1.0, gb_sb[:], ALU.add, ALU.mult)
+        nc.vector.scalar_tensor_tensor(ga_sgn[:], twice_pos[:], -1.0, ga_sb[:], ALU.add, ALU.mult)
+        nc.vector.tensor_scalar(ga_z[:], ga_sgn[:], 1.0 - C, None, ALU.mult)
+        for t in range(PACK):
+            b_gather(t)
+        for t in range(PACK):
+            a_finish(t)
+
+        z2_g = keep.tile([P, PACK * N], BF16, name="z2_g", align_bytes=64)
+        nc.scalar.copy(
+            z2_g[:].rearrange("p (c i t) -> p c t i", i=4, t=PACK),
+            z2b[:].rearrange("p t (c i) -> p c t i", i=4),
+        )
+        z_g = keep.tile([P, PACK * N], BF16, name="z_g", align_bytes=64)
+        deal(nc.vector.tensor_copy, z_g, zb[:], 0)
+        deal(nc.vector.tensor_copy, z_g, zb[:], 1)
+        z2_q = quantise("z2q", z2_g)
+        z_q = quantise("zq", z_g)
+
+        out_rows = out.rearrange("(p t) v -> p t v", t=PACK)
+        for t in range(PACK):
+            acc = product(z_q, t, z2_q[0], z2_q[1])
+            nc.scalar.activation(out=a_win[t][:, :N], in_=acc[:], func=ACT.Copy, scale=0.0625)
+        for t in range(PACK):
+            first = ring.tile([P, N], F32, name="first")
+            second = ring.tile([P, N], F32, name="second")
+            res = ring.tile([P, N], F32, name="res")
+            nc.vector.tensor_tensor(first[:], tab_win[t][:].indirect(l_n4[:]), a_win[t][:, :N], ALU.add)
+            nc.vector.tensor_copy(second[:], a_win[t][:].indirect(l_n5[:]))
+            nc.vector.tensor_tensor(res[:], first[:], second[:], ALU.max)
+            nc.sync.dma_start(out=out_rows[:, t, :], in_=res[:])

@@ -15,11 +15,16 @@ ACT = mybir.ActivationFunctionType
 
 P = 128
 PACK = 4
+LAST = PACK - 1
 N = 512
-T = 2048
-WIN = 2 * N
+HALF = N // 2
+TOKENS = 2048
+GROUP = 16
+QUADRANT = 32
 C = 0.3125
-FLOPS = 3 * 2 * 512 * 512 * 512
+KAPPA = (1.0 - C) / C
+BETA = 2.0 * C / (1.0 - 2.0 * C)
+FLOPS = 3 * 2 * N * N * N
 
 
 def tile_picked_kqstdtwicpkind_none_p_kernel(tc, x_words, x_scales, w1, w2, ga, gb, tab, offs, two, n1, n2, n3, n4, n5, out):
@@ -27,33 +32,33 @@ def tile_picked_kqstdtwicpkind_none_p_kernel(tc, x_words, x_scales, w1, w2, ga, 
     with ExitStack() as ctx:
         keep = ctx.enter_context(tc.tile_pool(name="keep", bufs=1))
         ring = ctx.enter_context(tc.tile_pool(name="ring", bufs=2))
-        psum = ctx.enter_context(tc.psum_pool(name="psum", bufs=2))
+        psum = ctx.enter_context(tc.psum_pool(name="psum", bufs=8))
 
-        def list_tile(name):
-            return keep.tile([P, N // 16], U16, name=name)
-
-        l_offs, l_two, l_n1, l_n2, l_n3, l_n4, l_n5 = [list_tile(n) for n in ("l_offs", "l_two", "l_n1", "l_n2", "l_n3", "l_n4", "l_n5")]
-        xs = keep.tile([P, T], U8, name="xs", align_bytes=64)
-        xw = keep.tile([P, T], U32, name="xw", align_bytes=64)
+        l_offs, l_two, l_n1, l_n2, l_n3, l_n4, l_n5 = [
+            keep.tile([P, N // GROUP], U16, name=name) for name in ("l_offs", "l_two", "l_n1", "l_n2", "l_n3", "l_n4", "l_n5")
+        ]
+        xs = keep.tile([P, TOKENS], U8, name="xs", align_bytes=64)
+        xw = keep.tile([P, TOKENS], U32, name="xw", align_bytes=64)
         w1_raw = keep.tile([P, PACK, N], F32, name="w1_raw")
         w2_raw = keep.tile([P, PACK, N], F32, name="w2_raw")
-        a_win = [keep.tile([P, WIN], F32, name="a_win%d" % t) for t in range(PACK)]
-        b_win = [keep.tile([P, WIN], F32, name="b_win%d" % t) for t in range(PACK)]
-        st_win = [keep.tile([P, WIN], F32, name="st_win%d" % t) for t in range(PACK)]
-        tab_win = [keep.tile([P, WIN], F32, name="tab_win%d" % t) for t in range(PACK)]
+        a_win = [keep.tile([P, 2 * N], F32, name="a_win%d" % t) for t in range(PACK)]
+        b_win = [keep.tile([P, 2 * N], F32, name="b_win%d" % t, align_bytes=64) for t in range(PACK)]
+        st_win = [keep.tile([P, 2 * N], F32, name="st_win%d" % t) for t in range(PACK)]
+        tab_win = [keep.tile([P, 2 * N], F32, name="tab_win%d" % t) for t in range(PACK)]
         ga_sb = keep.tile([P, PACK], F32, name="ga_sb")
         gb_sb = keep.tile([P, PACK], F32, name="gb_sb")
-        quarter = keep.tile([P, 1], F32, name="quarter")
-        warm = keep.tile([P, 1], F32, name="warm")
+        zero = keep.tile([P, 1], F32, name="zero")
         ident = keep.tile([P, P], F32, name="ident")
 
-        nc.vector.memset(xs[:].bitcast(I32), 0)
-        nc.vector.memset(quarter[:], 0.25)
-        nc.scalar.activation(out=warm[:], in_=quarter[:], func=ACT.Sigmoid)
+        nc.gpsimd.memset(xs[:].bitcast(I32), 0)
+        nc.vector.memset(zero[:], 0.0)
+        nc.scalar.activation(out=a_win[0][:, N:], in_=zero[:].to_broadcast([P, N]), func=ACT.Sigmoid)
         nc.sync.dma_start(l_offs[:], offs)
         nc.sync.dma_start(l_two[:], two)
-        for q in range(4):
-            nc.sync.dma_start(out=xs[32 * q : 32 * q + 4, :].bitcast(I32), in_=x_scales[0, 4 * q : 4 * q + 4, :].bitcast(I32))
+        for q in range(P // QUADRANT):
+            nc.sync.dma_start(
+                out=xs[QUADRANT * q : QUADRANT * q + PACK, :].bitcast(I32), in_=x_scales[0, PACK * q : PACK * (q + 1), :].bitcast(I32)
+            )
         nc.sync.dma_start(out=w1_raw[:], in_=w1.rearrange("(p j) c -> p j c", j=PACK))
         nc.sync.dma_start(out=xw[:].bitcast(I32), in_=x_words[0].rearrange("p n t -> p (n t)").bitcast(I32))
         nc.sync.dma_start(out=w2_raw[:], in_=w2.rearrange("(p j) c -> p j c", j=PACK))
@@ -68,144 +73,228 @@ def tile_picked_kqstdtwicpkind_none_p_kernel(tc, x_words, x_scales, w1, w2, ga, 
             nc.sync.dma_start(out=tab_win[t][:, :N], in_=tab_rows[:, t, :])
         nc.sync.dma_start(l_n4[:], n4)
         nc.sync.dma_start(l_n5[:], n5)
-        for t in range(PACK):
-            nc.vector.memset(b_win[t][:, N:], 0.0)
-        for t in range(PACK):
-            nc.vector.memset(tab_win[t][:, N:], 0.0)
 
-        xa_s = keep.tile([P, N], U8, name="xa_s", align_bytes=64)
-        xb_s = keep.tile([P, N], U8, name="xb_s", align_bytes=64)
-        xa_w = keep.tile([P, N], U32, name="xa_w", align_bytes=64)
-        xb_w = keep.tile([P, N], U32, name="xb_w", align_bytes=64)
-        nc.vector.tensor_copy(xa_s[:], xs[:].indirect(l_offs[:]))
-        nc.vector.tensor_copy(xb_s[:], xs[:].indirect(l_two[:]))
-
-        twice_pos = keep.tile([P, PACK], F32, name="twice_pos")
-        gb_abs = keep.tile([P, PACK], F32, name="gb_abs")
-        ga_sgn = keep.tile([P, PACK], F32, name="ga_sgn")
-        ga_z = keep.tile([P, PACK], F32, name="ga_z")
-
-        def deal(engine_copy, dst, src, half):
-            ms = slice(half * 64, (half + 1) * 64)
-            engine_copy(
-                dst[:].rearrange("p (t m j) -> p m j t", t=PACK, j=PACK)[:, ms, :, :],
-                src.rearrange("p j (m t) -> p m j t", t=PACK)[:, ms, :, :],
+        def deal(copy, grouped, rows, m0, m1):
+            copy(
+                grouped[:].rearrange("p (t m j) -> p m j t", t=PACK, j=PACK)[:, m0:m1, :, :],
+                rows.rearrange("p j (m t) -> p m j t", t=PACK)[:, m0:m1, :, :],
             )
 
-        def quantise(name, grouped):
-            codes = keep.tile([P, N], U32, name=name + "_c", align_bytes=64)
-            scales = keep.tile([P, N], U8, name=name + "_s", align_bytes=64)
-            nc.vector.quantize_mx(out=codes[:].bitcast(FP8X4), scales=scales[:], in_=grouped[:])
-            return codes, scales
+        def mx_tiles(name):
+            return keep.tile([P, N], U32, name=name + "_words", align_bytes=64), keep.tile([P, N], U8, name=name + "_scales", align_bytes=64)
 
-        def product(lhs, t, rhs_c, rhs_s):
-            acc = psum.tile([P, N], F32, name="acc")
-            cols = slice(t * P, (t + 1) * P)
-            nc.tensor.matmul_mx(out=acc[:], lhsT=lhs[0][:, cols].bitcast(FP8X4), lhsT_scale=lhs[1][:, cols],
-                                rhs=rhs_c[:].bitcast(FP8X4), rhs_scale=rhs_s[:], start=True, stop=True)
-            return acc
+        def quantise(mx, cols, grouped):
+            nc.vector.quantize_mx(out=mx[0][:, cols].bitcast(FP8X4), scales=mx[1][:, cols], in_=grouped)
 
-        def turned_sum(name, terms):
-            acc = psum.tile([P, N], F32, name=name)
-            for k in range(PACK):
-                cols = slice(k * P, (k + 1) * P)
+        def product(lhs, t, rhs, cols):
+            bank = psum.tile([P, cols.stop - cols.start], F32, name="bank")
+            rows = slice(t * P, (t + 1) * P)
+            nc.tensor.matmul_mx(
+                out=bank[:], lhsT=lhs[0][:, rows].bitcast(FP8X4), lhsT_scale=lhs[1][:, rows],
+                rhs=rhs[0][:, cols].bitcast(FP8X4), rhs_scale=rhs[1][:, cols], start=True, stop=True,
+            )
+            return bank
+
+        def turned_sum(terms):
+            bank = psum.tile([P, N], F32, name="bank")
+            for block in range(N // P):
+                cols = slice(block * P, (block + 1) * P)
                 for i, term in enumerate(terms):
-                    nc.tensor.matmul(acc[:, cols], term[:, cols], ident[:], start=(i == 0), stop=(i == len(terms) - 1), is_transpose=True)
-            return acc
+                    nc.tensor.matmul(bank[:, cols], term[:, cols], ident[:], start=(i == 0), stop=(i == len(terms) - 1), is_transpose=True)
+            return bank
 
+        every = slice(0, N)
+        halves = [slice(0, HALF), slice(HALF, N)]
+
+        x_a = mx_tiles("x_a")
+        x_b = mx_tiles("x_b")
+        nc.vector.tensor_copy(x_a[1][:], xs[:].indirect(l_offs[:]))
+        nc.vector.tensor_copy(x_b[1][:], xs[:].indirect(l_two[:]))
         w1_g = keep.tile([P, PACK * N], BF16, name="w1_g", align_bytes=64)
         w2_g = keep.tile([P, PACK * N], BF16, name="w2_g", align_bytes=64)
-        deal(nc.scalar.copy, w1_g, w1_raw[:], 0)
-        deal(nc.vector.tensor_copy, w1_g, w1_raw[:], 1)
-        w1_q = quantise("w1q", w1_g)
-        nc.vector.tensor_copy(xa_w[:], xw[:].indirect(l_offs[:]))
-        nc.vector.tensor_copy(xb_w[:], xw[:].indirect(l_two[:]))
+        deal(nc.scalar.copy, w1_g, w1_raw[:], 0, P // 2)
+        deal(nc.vector.tensor_copy, w1_g, w1_raw[:], P // 2, P)
+        w1_q = mx_tiles("w1_q")
+        quantise(w1_q, every, w1_g[:])
+        nc.vector.tensor_copy(x_a[0][:], xw[:].indirect(l_offs[:]))
+        nc.vector.tensor_copy(x_b[0][:], xw[:].indirect(l_two[:]))
 
-        num = keep.tile([P, PACK, N], F32, name="num")
-        sq_d = keep.tile([P, PACK, N], F32, name="sq_d")
+        a_kappa = [a_win[1][:, N:], a_win[2][:, N:], a_win[3][:, N:], b_win[0][:, N:]]
+        a_rest_late = keep.tile([P, 2, N], F32, name="a_rest_late")
+        a_rest = [b_win[1][:, N:], b_win[2][:, N:], a_rest_late[:, 0, :], a_rest_late[:, 1, :]]
+        n_sum = [tab_win[t][:, N:] for t in range(PACK)]
+        g = [b_win[LAST][:, N:]] + [keep.tile([P, N], F32, name="g%d" % t, align_bytes=64)[:] for t in range(1, PACK)]
+        sig = [st_win[(t - 1) % PACK][:, N:] for t in range(PACK)]
+        u = [keep.tile([P, N], F32, name=name, align_bytes=64) for name in ("u0", "w2_g", "u2", "u3")]
+        quarter = b_win[LAST][:, N : N + 1]
+        st_far = [ring.tile([P, N], F32, name="st_far") for t in range(PACK)]
+        sq_d = [keep.tile([P, N], F32, name="sq_d%d" % t, align_bytes=64) for t in range(PACK)]
         sq_e = keep.tile([P, PACK, N], F32, name="sq_e")
-        zb = keep.tile([P, PACK, N], BF16, name="zb")
-        z2b = keep.tile([P, PACK, N], BF16, name="z2b")
+        inv_root = keep.tile([P, PACK, N], F32, name="inv_root")
+        z_rows = keep.tile([P, PACK, N], BF16, name="z_rows")
+        z2_rows = keep.tile([P, PACK, N], BF16, name="z2_rows")
+        gb_step = keep.tile([P, PACK], F32, name="gb_step")
+        gb_abs = keep.tile([P, PACK], F32, name="gb_abs")
+        ga_z = keep.tile([P, PACK], F32, name="ga_z")
+        w2_q = mx_tiles("w2_q")
 
         def a_out(t):
-            acc = product(w1_q, t, xa_w, xa_s)
-            nc.scalar.copy(a_win[t][:, :N], acc[:])
-            nc.scalar.activation(out=a_win[t][:, N:], in_=acc[:], func=ACT.Copy, scale=-2.0 * C / (1.0 - 2.0 * C))
+            bank = product(w1_q, t, x_a, every)
+            nc.scalar.copy(a_win[t][:, :N], bank[:])
+            if t == 0:
+                nc.vector.tensor_scalar(a_kappa[t], a_win[t][:, :N], KAPPA, None, ALU.mult)
+            else:
+                nc.scalar.activation(out=a_kappa[t], in_=bank[:], func=ACT.Copy, scale=KAPPA)
 
-        def a_gather(t):
-            pa = ring.tile([P, N], F32, name="pa")
-            diff = ring.tile([P, N], F32, name="diff")
-            both = ring.tile([P, N], F32, name="both")
-            nc.vector.tensor_copy(pa[:], a_win[t][:].indirect(l_n1[:]))
-            nc.vector.tensor_tensor(diff[:], a_win[t][:].indirect(l_n2[:]), pa[:], ALU.subtract)
-            nc.vector.scalar_tensor_tensor(both[:], pa[:], 2.0, diff[:], ALU.mult, ALU.add)
-            nc.vector.scalar_tensor_tensor(num[:, t, :], both[:], -C / (1.0 - C), a_win[t][:, :N], ALU.mult, ALU.add)
-            d_t = turned_sum("d_t", [diff])
-            e_t = turned_sum("e_t", [both, a_win[t][:, N:]])
-            nc.scalar.activation(out=sq_d[:, t, :], in_=d_t[:], func=ACT.Square)
-            nc.scalar.activation(out=sq_e[:, t, :], in_=e_t[:], func=ACT.Square, scale=1.0 - 2.0 * C)
+        def a_scale_rest(t):
+            nc.scalar.activation(out=a_rest[t], in_=a_win[t][:, :N], func=ACT.Copy, scale=KAPPA - BETA)
 
-        def b_out(t, w2_q):
-            acc = product(w2_q, t, xb_w, xb_s)
-            nc.scalar.copy(b_win[t][:, :N], acc[:])
-            nc.scalar.activation(out=st_win[t][:, N:], in_=b_win[t][:].indirect(l_n3[:]), func=ACT.Sigmoid)
+        def fetch_g(t):
+            nc.vector.tensor_tensor(g[t], a_win[t][:].indirect(l_n1[:]), a_kappa[t], ALU.subtract)
 
-        def b_gather(t):
-            other = ring.tile([P, N], F32, name="other")
-            nc.vector.scalar_tensor_tensor(st_win[t][:, :N], b_win[t][:, :N], gb_abs[:, t : t + 1], st_win[t][:, N:], ALU.mult, ALU.mult)
-            nc.vector.tensor_copy(other[:], st_win[t][:].indirect(l_n3[:]))
-            nc.vector.tensor_tensor(z2b[:, t, :], other[:], st_win[t][:, :N], ALU.max)
+        def fetch_n(t):
+            nc.vector.tensor_tensor(n_sum[t], a_win[t][:].indirect(l_n2[:]), g[t], ALU.add)
 
-        def a_finish(t):
-            den = turned_sum("den", [sq_d[:, t, :], sq_e[:, t, :]])
-            rs = ring.tile([P, N], F32, name="rs")
-            nc.scalar.activation(out=rs[:], in_=den[:], func=ACT.Abs_reciprocal_sqrt, bias=quarter[:], scale=0.5)
-            nc.vector.scalar_tensor_tensor(zb[:, t, :], num[:, t, :], ga_z[:, t : t + 1], rs[:], ALU.mult, ALU.mult)
+        def make_u(t):
+            nc.vector.scalar_tensor_tensor(u[t][:], g[t], 2.0, n_sum[t], ALU.mult, ALU.subtract)
+
+        def fetch_pair(t):
+            fetch_g(t)
+            fetch_n(t)
+            fetch_g(t + 1)
+            make_u(t)
+            fetch_n(t + 1)
+
+        def turn_e_d(t):
+            return turned_sum([n_sum[t], a_rest[t]]), turned_sum([u[t], a_kappa[t]])
+
+        def square(t, e_d):
+            nc.scalar.activation(out=sq_e[:, t, :], in_=e_d[0][:], func=ACT.Square, scale=1.0 - 2.0 * C)
+            nc.scalar.activation(out=sq_d[t][:], in_=e_d[1][:], func=ACT.Square)
+
+        def root(t):
+            bank = turned_sum([sq_e[:, t, :], sq_d[t]])
+            nc.scalar.activation(out=inv_root[:, t, :], in_=bank[:], func=ACT.Abs_reciprocal_sqrt, bias=quarter, scale=0.5)
+
+        def b_out(t, bank):
+            nc.scalar.copy(b_win[t][:, :N], bank[:])
+            nc.scalar.activation(out=sig[t], in_=b_win[t][:].indirect(l_n3[:]), func=ACT.Sigmoid)
+
+        def make_st(t):
+            nc.vector.scalar_tensor_tensor(st_win[t][:, :N], b_win[t][:, :N], gb_abs[:, t : t + 1], sig[t], ALU.mult, ALU.mult)
+
+        def fetch_st(t):
+            nc.vector.tensor_copy(st_far[t][:], st_win[t][:].indirect(l_n3[:]))
+
+        def make_z2(t):
+            nc.vector.tensor_tensor(z2_rows[:, t, :], st_far[t][:], st_win[t][:, :N], ALU.max)
 
         a_out(0)
         a_out(1)
-        deal(nc.scalar.copy, w2_g, w2_raw[:], 0)
-        deal(nc.scalar.copy, w2_g, w2_raw[:], 1)
-        a_gather(0)
+        deal(nc.scalar.copy, w2_g, w2_raw[:], 0, P)
         a_out(2)
-        w2_q = quantise("w2q", w2_g)
-        a_gather(1)
         a_out(3)
-        b_out(0, w2_q)
-        a_gather(2)
-        b_out(1, w2_q)
-        a_gather(3)
-        b_out(2, w2_q)
-        b_out(3, w2_q)
-        nc.vector.tensor_scalar(twice_pos[:], gb_sb[:], 0.0, 2.0, ALU.is_ge, ALU.mult)
-        nc.vector.scalar_tensor_tensor(gb_abs[:], twice_pos[:], -1.0, gb_sb[:], ALU.add, ALU.mult)
-        nc.vector.scalar_tensor_tensor(ga_sgn[:], twice_pos[:], -1.0, ga_sb[:], ALU.add, ALU.mult)
-        nc.vector.tensor_scalar(ga_z[:], ga_sgn[:], 1.0 - C, None, ALU.mult)
-        for t in range(PACK):
-            b_gather(t)
-        for t in range(PACK):
-            a_finish(t)
+        a_scale_rest(0)
+        a_scale_rest(1)
 
-        z2_g = keep.tile([P, PACK * N], BF16, name="z2_g", align_bytes=64)
-        nc.scalar.copy(
-            z2_g[:].rearrange("p (c i t) -> p c t i", i=4, t=PACK),
-            z2b[:].rearrange("p t (c i) -> p c t i", i=4),
-        )
+        fetch_pair(0)
+        quantise(w2_q, every, w2_g[:])
+        b_banks = [product(w2_q, t, x_b, every) for t in range(PACK)]
+        make_u(1)
+        fetch_pair(2)
+        nc.vector.tensor_scalar(gb_step[:], gb_sb[:], 0.0, -2.0 * C, ALU.is_ge, ALU.mult)
+        nc.vector.scalar_tensor_tensor(gb_abs[:], gb_sb[:], -1.0, gb_sb[:], ALU.mult, ALU.max)
+        nc.vector.scalar_tensor_tensor(ga_z[:], gb_step[:], C, ga_sb[:], ALU.add, ALU.mult)
+        make_u(LAST)
+
+        b_out(0, b_banks[0])
+        b_out(1, b_banks[1])
+        e_d = [turn_e_d(0), turn_e_d(1)]
+        a_scale_rest(2)
+        e_d.append(turn_e_d(2))
+        square(0, e_d[0])
+        b_out(2, b_banks[2])
+        a_scale_rest(LAST)
+        b_out(LAST, b_banks[LAST])
+        nc.gpsimd.memset(quarter, 0.25)
+        e_d.append(turn_e_d(LAST))
+        for t in range(1, PACK):
+            square(t, e_d[t])
+            root(t - 1)
+        root(LAST)
+
+        make_st(0)
+        for t in range(LAST - 1):
+            make_st(t + 1)
+            fetch_st(t)
+            make_z2(t)
+        make_st(LAST)
+        for step in (fetch_st, make_z2):
+            step(LAST - 1)
+            step(LAST)
+
+        z2_g = [b_win[LAST][:, N:].bitcast(BF16), keep.tile([P, PACK * HALF], BF16, name="sq_d%d" % LAST, align_bytes=64)[:]]
+        for h in range(2):
+            nc.scalar.copy(
+                z2_g[h].rearrange("p (c i t) -> p c t i", i=4, t=PACK),
+                z2_rows[:, :, halves[h]].rearrange("p t (c i) -> p c t i", i=4),
+            )
+        for t in range(PACK):
+            nc.vector.scalar_tensor_tensor(z_rows[:, t, :], n_sum[t], ga_z[:, t : t + 1], inv_root[:, t, :], ALU.mult, ALU.mult)
         z_g = keep.tile([P, PACK * N], BF16, name="z_g", align_bytes=64)
-        deal(nc.vector.tensor_copy, z_g, zb[:], 0)
-        deal(nc.vector.tensor_copy, z_g, zb[:], 1)
-        z2_q = quantise("z2q", z2_g)
-        z_q = quantise("zq", z_g)
+        deal(nc.vector.tensor_copy, z_g, z_rows[:], 0, P)
+
+        z_q = mx_tiles("z_q")
+        z2_q = mx_tiles("z2_q")
+        quantise(z2_q, halves[0], z2_g[0])
+        quantise(z_q, slice(0, P), z_g[:, :N])
+        quantise(z2_q, halves[1], z2_g[1])
+        for t in range(1, PACK):
+            quantise(z_q, slice(t * P, (t + 1) * P), z_g[:, t * N : (t + 1) * N])
+
+        def s_out(t, cols, bank):
+            nc.scalar.activation(out=a_win[t][:, cols], in_=bank[:], func=ACT.Copy, scale=0.0625)
+
+        for cols in halves:
+            s_out(0, cols, product(z_q, 0, z2_q, cols))
+        s_banks = [product(z_q, t, z2_q, every) for t in range(1, PACK)]
+        for t in range(1, PACK):
+            s_out(t, every, s_banks[t - 1])
 
         out_rows = out.rearrange("(p t) v -> p t v", t=PACK)
-        for t in range(PACK):
-            acc = product(z_q, t, z2_q[0], z2_q[1])
-            nc.scalar.activation(out=a_win[t][:, :N], in_=acc[:], func=ACT.Copy, scale=0.0625)
-        for t in range(PACK):
-            first = ring.tile([P, N], F32, name="first")
-            second = ring.tile([P, N], F32, name="second")
-            res = ring.tile([P, N], F32, name="res")
-            nc.vector.tensor_tensor(first[:], tab_win[t][:].indirect(l_n4[:]), a_win[t][:, :N], ALU.add)
-            nc.vector.tensor_copy(second[:], a_win[t][:].indirect(l_n5[:]))
-            nc.vector.tensor_tensor(res[:], first[:], second[:], ALU.max)
-            nc.sync.dma_start(out=out_rows[:, t, :], in_=res[:])
+        s_tab = [keep.tile([P, N], F32, name="s_tab%d" % t) for t in range(PACK)]
+        s_far = [keep.tile([P, N], F32, name="s_far%d" % t) for t in range(1, PACK)]
+        result = [keep.tile([P, N], F32, name="result%d" % t) for t in range(PACK)]
+
+        def fetch_tab(t, cols):
+            entries = l_n4[:, cols.start // GROUP : cols.stop // GROUP]
+            nc.vector.tensor_tensor(s_tab[t][:, cols], tab_win[t][:].indirect(entries), a_win[t][:, cols], ALU.add)
+
+        def fetch_s(t):
+            nc.vector.tensor_copy(s_far[t - 1][:], a_win[t][:].indirect(l_n5[:]))
+
+        def finish(t, cols):
+            nc.vector.tensor_tensor(result[t][:, cols], s_tab[t][:, cols], s_far[t - 1][:, cols], ALU.max)
+            nc.sync.dma_start(out=out_rows[:, t, cols], in_=result[t][:, cols])
+
+        for cols in halves:
+            fetch_tab(0, cols)
+        excess = keep.tile([P, N], F32, name="excess")
+        excess_pos = keep.tile([P, N], F32, name="excess_pos")
+        turned = keep.tile([P, N], F32, name="turned")
+        nc.vector.tensor_tensor(excess[:], a_win[0][:].indirect(l_n5[:]), s_tab[0][:], ALU.subtract)
+        nc.scalar.activation(out=excess_pos[:], in_=excess[:], func=ACT.Relu)
+        nc.scalar.copy(turned[:], turned_sum([s_tab[0], excess_pos])[:])
+        nc.scalar.copy(result[0][:], turned_sum([turned])[:])
+        nc.scalar.dma_start(out=out_rows[:, 0, :], in_=result[0][:])
+
+        fetch_tab(1, every)
+        fetch_s(1)
+        fetch_tab(2, every)
+        finish(1, every)
+        fetch_s(2)
+        fetch_tab(LAST, every)
+        fetch_s(LAST)
+        finish(2, every)
+        for cols in halves:
+            finish(LAST, cols)

from contextlib import ExitStack

import concourse.mybir as mybir
from concourse.masks import make_identity

F32 = mybir.dt.float32
BF16 = mybir.dt.bfloat16
I32 = mybir.dt.int32
U32 = mybir.dt.uint32
U16 = mybir.dt.uint16
U8 = mybir.dt.uint8
FP8X4 = mybir.dt.float8_e4m3fn_x4
ALU = mybir.AluOpType
ACT = mybir.ActivationFunctionType

P = 128
PACK = 4
LAST = PACK - 1
N = 512
HALF = N // 2
TOKENS = 2048
GROUP = 16
QUADRANT = 32
C = 0.3125
KAPPA = (1.0 - C) / C
BETA = 2.0 * C / (1.0 - 2.0 * C)
FLOPS = 3 * 2 * N * N * N


def tile_picked_kqstdtwicpkind_none_p_kernel(tc, x_words, x_scales, w1, w2, ga, gb, tab, offs, two, n1, n2, n3, n4, n5, out):
    nc = tc.nc
    with ExitStack() as ctx:
        keep = ctx.enter_context(tc.tile_pool(name="keep", bufs=1))
        ring = ctx.enter_context(tc.tile_pool(name="ring", bufs=2))
        psum = ctx.enter_context(tc.psum_pool(name="psum", bufs=8))

        l_offs, l_two, l_n1, l_n2, l_n3, l_n4, l_n5 = [
            keep.tile([P, N // GROUP], U16, name=name) for name in ("l_offs", "l_two", "l_n1", "l_n2", "l_n3", "l_n4", "l_n5")
        ]
        xs = keep.tile([P, TOKENS], U8, name="xs", align_bytes=64)
        xw = keep.tile([P, TOKENS], U32, name="xw", align_bytes=64)
        w1_raw = keep.tile([P, PACK, N], F32, name="w1_raw")
        w2_raw = keep.tile([P, PACK, N], F32, name="w2_raw")
        a_win = [keep.tile([P, 2 * N], F32, name="a_win%d" % t) for t in range(PACK)]
        b_win = [keep.tile([P, 2 * N], F32, name="b_win%d" % t, align_bytes=64) for t in range(PACK)]
        st_win = [keep.tile([P, 2 * N], F32, name="st_win%d" % t) for t in range(PACK)]
        tab_win = [keep.tile([P, 2 * N], F32, name="tab_win%d" % t) for t in range(PACK)]
        ga_sb = keep.tile([P, PACK], F32, name="ga_sb")
        gb_sb = keep.tile([P, PACK], F32, name="gb_sb")
        zero = keep.tile([P, 1], F32, name="zero")
        ident = keep.tile([P, P], F32, name="ident")

        nc.gpsimd.memset(xs[:].bitcast(I32), 0)
        nc.vector.memset(zero[:], 0.0)
        nc.scalar.activation(out=a_win[0][:, N:], in_=zero[:].to_broadcast([P, N]), func=ACT.Sigmoid)
        nc.sync.dma_start(l_offs[:], offs)
        nc.sync.dma_start(l_two[:], two)
        for q in range(P // QUADRANT):
            nc.sync.dma_start(
                out=xs[QUADRANT * q : QUADRANT * q + PACK, :].bitcast(I32), in_=x_scales[0, PACK * q : PACK * (q + 1), :].bitcast(I32)
            )
        nc.sync.dma_start(out=w1_raw[:], in_=w1.rearrange("(p j) c -> p j c", j=PACK))
        nc.sync.dma_start(out=xw[:].bitcast(I32), in_=x_words[0].rearrange("p n t -> p (n t)").bitcast(I32))
        nc.sync.dma_start(out=w2_raw[:], in_=w2.rearrange("(p j) c -> p j c", j=PACK))
        nc.sync.dma_start(l_n1[:], n1)
        nc.sync.dma_start(l_n2[:], n2)
        nc.sync.dma_start(l_n3[:], n3)
        nc.sync.dma_start(out=ga_sb[:], in_=ga.rearrange("(p t) o -> p (t o)", t=PACK))
        nc.sync.dma_start(out=gb_sb[:], in_=gb.rearrange("(p t) o -> p (t o)", t=PACK))
        make_identity(nc, ident[:])
        tab_rows = tab.rearrange("(p t) v -> p t v", t=PACK)
        for t in range(PACK):
            nc.sync.dma_start(out=tab_win[t][:, :N], in_=tab_rows[:, t, :])
        nc.sync.dma_start(l_n4[:], n4)
        nc.sync.dma_start(l_n5[:], n5)

        def deal(copy, grouped, rows, m0, m1):
            copy(
                grouped[:].rearrange("p (t m j) -> p m j t", t=PACK, j=PACK)[:, m0:m1, :, :],
                rows.rearrange("p j (m t) -> p m j t", t=PACK)[:, m0:m1, :, :],
            )

        def mx_tiles(name):
            return keep.tile([P, N], U32, name=name + "_words", align_bytes=64), keep.tile([P, N], U8, name=name + "_scales", align_bytes=64)

        def quantise(mx, cols, grouped):
            nc.vector.quantize_mx(out=mx[0][:, cols].bitcast(FP8X4), scales=mx[1][:, cols], in_=grouped)

        def product(lhs, t, rhs, cols):
            bank = psum.tile([P, cols.stop - cols.start], F32, name="bank")
            rows = slice(t * P, (t + 1) * P)
            nc.tensor.matmul_mx(
                out=bank[:], lhsT=lhs[0][:, rows].bitcast(FP8X4), lhsT_scale=lhs[1][:, rows],
                rhs=rhs[0][:, cols].bitcast(FP8X4), rhs_scale=rhs[1][:, cols], start=True, stop=True,
            )
            return bank

        def turned_sum(terms):
            bank = psum.tile([P, N], F32, name="bank")
            for block in range(N // P):
                cols = slice(block * P, (block + 1) * P)
                for i, term in enumerate(terms):
                    nc.tensor.matmul(bank[:, cols], term[:, cols], ident[:], start=(i == 0), stop=(i == len(terms) - 1), is_transpose=True)
            return bank

        every = slice(0, N)
        halves = [slice(0, HALF), slice(HALF, N)]

        x_a = mx_tiles("x_a")
        x_b = mx_tiles("x_b")
        nc.vector.tensor_copy(x_a[1][:], xs[:].indirect(l_offs[:]))
        nc.vector.tensor_copy(x_b[1][:], xs[:].indirect(l_two[:]))
        w1_g = keep.tile([P, PACK * N], BF16, name="w1_g", align_bytes=64)
        w2_g = keep.tile([P, PACK * N], BF16, name="w2_g", align_bytes=64)
        deal(nc.scalar.copy, w1_g, w1_raw[:], 0, P // 2)
        deal(nc.vector.tensor_copy, w1_g, w1_raw[:], P // 2, P)
        w1_q = mx_tiles("w1_q")
        quantise(w1_q, every, w1_g[:])
        nc.vector.tensor_copy(x_a[0][:], xw[:].indirect(l_offs[:]))
        nc.vector.tensor_copy(x_b[0][:], xw[:].indirect(l_two[:]))

        a_kappa = [a_win[1][:, N:], a_win[2][:, N:], a_win[3][:, N:], b_win[0][:, N:]]
        a_rest_late = keep.tile([P, 2, N], F32, name="a_rest_late")
        a_rest = [b_win[1][:, N:], b_win[2][:, N:], a_rest_late[:, 0, :], a_rest_late[:, 1, :]]
        n_sum = [tab_win[t][:, N:] for t in range(PACK)]
        g = [b_win[LAST][:, N:]] + [keep.tile([P, N], F32, name="g%d" % t, align_bytes=64)[:] for t in range(1, PACK)]
        sig = [st_win[(t - 1) % PACK][:, N:] for t in range(PACK)]
        u = [keep.tile([P, N], F32, name=name, align_bytes=64) for name in ("u0", "w2_g", "u2", "u3")]
        quarter = b_win[LAST][:, N : N + 1]
        st_far = [ring.tile([P, N], F32, name="st_far") for t in range(PACK)]
        sq_d = [keep.tile([P, N], F32, name="sq_d%d" % t, align_bytes=64) for t in range(PACK)]
        sq_e = keep.tile([P, PACK, N], F32, name="sq_e")
        inv_root = keep.tile([P, PACK, N], F32, name="inv_root")
        z_rows = keep.tile([P, PACK, N], BF16, name="z_rows")
        z2_rows = keep.tile([P, PACK, N], BF16, name="z2_rows")
        gb_step = keep.tile([P, PACK], F32, name="gb_step")
        gb_abs = keep.tile([P, PACK], F32, name="gb_abs")
        ga_z = keep.tile([P, PACK], F32, name="ga_z")
        w2_q = mx_tiles("w2_q")

        def a_out(t):
            bank = product(w1_q, t, x_a, every)
            nc.scalar.copy(a_win[t][:, :N], bank[:])
            if t == 0:
                nc.vector.tensor_scalar(a_kappa[t], a_win[t][:, :N], KAPPA, None, ALU.mult)
            else:
                nc.scalar.activation(out=a_kappa[t], in_=bank[:], func=ACT.Copy, scale=KAPPA)

        def a_scale_rest(t):
            nc.scalar.activation(out=a_rest[t], in_=a_win[t][:, :N], func=ACT.Copy, scale=KAPPA - BETA)

        def fetch_g(t):
            nc.vector.tensor_tensor(g[t], a_win[t][:].indirect(l_n1[:]), a_kappa[t], ALU.subtract)

        def fetch_n(t):
            nc.vector.tensor_tensor(n_sum[t], a_win[t][:].indirect(l_n2[:]), g[t], ALU.add)

        def make_u(t):
            nc.vector.scalar_tensor_tensor(u[t][:], g[t], 2.0, n_sum[t], ALU.mult, ALU.subtract)

        def fetch_pair(t):
            fetch_g(t)
            fetch_n(t)
            fetch_g(t + 1)
            make_u(t)
            fetch_n(t + 1)

        def turn_e_d(t):
            return turned_sum([n_sum[t], a_rest[t]]), turned_sum([u[t], a_kappa[t]])

        def square(t, e_d):
            nc.scalar.activation(out=sq_e[:, t, :], in_=e_d[0][:], func=ACT.Square, scale=1.0 - 2.0 * C)
            nc.scalar.activation(out=sq_d[t][:], in_=e_d[1][:], func=ACT.Square)

        def root(t):
            bank = turned_sum([sq_e[:, t, :], sq_d[t]])
            nc.scalar.activation(out=inv_root[:, t, :], in_=bank[:], func=ACT.Abs_reciprocal_sqrt, bias=quarter, scale=0.5)

        def b_out(t, bank):
            nc.scalar.copy(b_win[t][:, :N], bank[:])
            nc.scalar.activation(out=sig[t], in_=b_win[t][:].indirect(l_n3[:]), func=ACT.Sigmoid)

        def make_st(t):
            nc.vector.scalar_tensor_tensor(st_win[t][:, :N], b_win[t][:, :N], gb_abs[:, t : t + 1], sig[t], ALU.mult, ALU.mult)

        def fetch_st(t):
            nc.vector.tensor_copy(st_far[t][:], st_win[t][:].indirect(l_n3[:]))

        def make_z2(t):
            nc.vector.tensor_tensor(z2_rows[:, t, :], st_far[t][:], st_win[t][:, :N], ALU.max)

        a_out(0)
        a_out(1)
        deal(nc.scalar.copy, w2_g, w2_raw[:], 0, P)
        a_out(2)
        a_out(3)
        a_scale_rest(0)
        a_scale_rest(1)

        fetch_pair(0)
        quantise(w2_q, every, w2_g[:])
        b_banks = [product(w2_q, t, x_b, every) for t in range(PACK)]
        make_u(1)
        fetch_pair(2)
        nc.vector.tensor_scalar(gb_step[:], gb_sb[:], 0.0, -2.0 * C, ALU.is_ge, ALU.mult)
        nc.vector.scalar_tensor_tensor(gb_abs[:], gb_sb[:], -1.0, gb_sb[:], ALU.mult, ALU.max)
        nc.vector.scalar_tensor_tensor(ga_z[:], gb_step[:], C, ga_sb[:], ALU.add, ALU.mult)
        make_u(LAST)

        b_out(0, b_banks[0])
        b_out(1, b_banks[1])
        e_d = [turn_e_d(0), turn_e_d(1)]
        a_scale_rest(2)
        e_d.append(turn_e_d(2))
        square(0, e_d[0])
        b_out(2, b_banks[2])
        a_scale_rest(LAST)
        b_out(LAST, b_banks[LAST])
        nc.gpsimd.memset(quarter, 0.25)
        e_d.append(turn_e_d(LAST))
        for t in range(1, PACK):
            square(t, e_d[t])
            root(t - 1)
        root(LAST)

        make_st(0)
        for t in range(LAST - 1):
            make_st(t + 1)
            fetch_st(t)
            make_z2(t)
        make_st(LAST)
        for step in (fetch_st, make_z2):
            step(LAST - 1)
            step(LAST)

        z2_g = [b_win[LAST][:, N:].bitcast(BF16), keep.tile([P, PACK * HALF], BF16, name="sq_d%d" % LAST, align_bytes=64)[:]]
        for h in range(2):
            nc.scalar.copy(
                z2_g[h].rearrange("p (c i t) -> p c t i", i=4, t=PACK),
                z2_rows[:, :, halves[h]].rearrange("p t (c i) -> p c t i", i=4),
            )
        for t in range(PACK):
            nc.vector.scalar_tensor_tensor(z_rows[:, t, :], n_sum[t], ga_z[:, t : t + 1], inv_root[:, t, :], ALU.mult, ALU.mult)
        z_g = keep.tile([P, PACK * N], BF16, name="z_g", align_bytes=64)
        deal(nc.vector.tensor_copy, z_g, z_rows[:], 0, P)

        z_q = mx_tiles("z_q")
        z2_q = mx_tiles("z2_q")
        quantise(z2_q, halves[0], z2_g[0])
        quantise(z_q, slice(0, P), z_g[:, :N])
        quantise(z2_q, halves[1], z2_g[1])
        for t in range(1, PACK):
            quantise(z_q, slice(t * P, (t + 1) * P), z_g[:, t * N : (t + 1) * N])

        def s_out(t, cols, bank):
            nc.scalar.activation(out=a_win[t][:, cols], in_=bank[:], func=ACT.Copy, scale=0.0625)

        for cols in halves:
            s_out(0, cols, product(z_q, 0, z2_q, cols))
        s_banks = [product(z_q, t, z2_q, every) for t in range(1, PACK)]
        for t in range(1, PACK):
            s_out(t, every, s_banks[t - 1])

        out_rows = out.rearrange("(p t) v -> p t v", t=PACK)
        s_tab = [keep.tile([P, N], F32, name="s_tab%d" % t) for t in range(PACK)]
        s_far = [keep.tile([P, N], F32, name="s_far%d" % t) for t in range(1, PACK)]
        result = [keep.tile([P, N], F32, name="result%d" % t) for t in range(PACK)]

        def fetch_tab(t, cols):
            entries = l_n4[:, cols.start // GROUP : cols.stop // GROUP]
            nc.vector.tensor_tensor(s_tab[t][:, cols], tab_win[t][:].indirect(entries), a_win[t][:, cols], ALU.add)

        def fetch_s(t):
            nc.vector.tensor_copy(s_far[t - 1][:], a_win[t][:].indirect(l_n5[:]))

        def finish(t, cols):
            nc.vector.tensor_tensor(result[t][:, cols], s_tab[t][:, cols], s_far[t - 1][:, cols], ALU.max)
            nc.sync.dma_start(out=out_rows[:, t, cols], in_=result[t][:, cols])

        for cols in halves:
            fetch_tab(0, cols)
        excess = keep.tile([P, N], F32, name="excess")
        excess_pos = keep.tile([P, N], F32, name="excess_pos")
        turned = keep.tile([P, N], F32, name="turned")
        nc.vector.tensor_tensor(excess[:], a_win[0][:].indirect(l_n5[:]), s_tab[0][:], ALU.subtract)
        nc.scalar.activation(out=excess_pos[:], in_=excess[:], func=ACT.Relu)
        nc.scalar.copy(turned[:], turned_sum([s_tab[0], excess_pos])[:])
        nc.scalar.copy(result[0][:], turned_sum([turned])[:])
        nc.scalar.dma_start(out=out_rows[:, 0, :], in_=result[0][:])

        fetch_tab(1, every)
        fetch_s(1)
        fetch_tab(2, every)
        finish(1, every)
        fetch_s(2)
        fetch_tab(LAST, every)
        fetch_s(LAST)
        finish(2, every)
        for cols in halves:
            finish(LAST, cols)
